import numpy as np
import ml_dtypes


def mxq(x, axis, fmt="e4m3"):
    dtype, down = {"e4m3": (ml_dtypes.float8_e4m3fn, 7), "e5m2": (ml_dtypes.float8_e5m2, 14)}[fmt]
    v = np.moveaxis(np.asarray(x, np.float32).astype(ml_dtypes.bfloat16).astype(np.float64), axis, -1)
    blocks = v.reshape(v.shape[:-1] + (-1, 32))
    amax = np.abs(blocks).max(-1, keepdims=True)
    byte = np.maximum(np.where(amax > 0, np.frexp(amax)[1] - 1 + 127, 0) - down, 1)
    scale = np.exp2(byte - 127.0)
    codes = (blocks / scale).astype(np.float32).astype(dtype).astype(np.float64)
    return np.moveaxis((codes * scale).reshape(v.shape), -1, axis)


WIDE = False


def mx_kscale(k):
    if not WIDE:
        return np.ones(k)
    levels = np.array([10, -10, 5, -5, 0])
    if k % 512:
        return np.exp2(np.random.permutation(np.resize(levels, k // 32))).repeat(32)
    a = np.empty((k // 512, 16))
    for p in range(k // 512):
        a[p, :8] = np.random.permutation(np.resize(levels, 8))
        for g in range(8):
            far = levels[np.abs(levels - a[p, g]) >= 10]
            a[p, g + 8] = far[np.random.randint(len(far))]
    return np.exp2(a.ravel()).repeat(32)


def f64(x):
    return np.asarray(x).astype(np.float64)


def striped(idx):
    return np.tile(idx.reshape(-1, 16).T, (8, 1)).astype(np.uint16)


def unstriped(offs):
    return offs[:16].T.reshape(-1).astype(np.int64)


K, T, D, S, V, N = 1536, 1024, 2, 512, 256, 128


def setup_inputs():
    n = np.random.standard_normal
    s = mx_kscale(K)[:, None]
    return {
        "xT": (n((K, T)) * s).astype(np.float32),
        "w": (n((D, K, N)) / np.sqrt(D * K) / s[None]).astype(np.float32),
        "gate": np.tile(np.random.uniform(0.2, 1.0, S), (N, 1)).astype(np.float32),
        "offs": striped(np.random.permutation(T)[:S]),
    }


def reference(xT, w, gate, offs):
    idx = unstriped(offs)
    xq = mxq(f64(xT)[:, idx], 0, "e4m3")
    wq = mxq(f64(w), 1, "e4m3")
    y = sum(wq[d].T @ xq[:, d * V:(d + 1) * V] for d in range(D))
    out = np.zeros((N, T))
    out[:, idx] = f64(gate) * np.tile(y, (1, D))
    return out

@@ -1,0 +1,169 @@
+from contextlib import ExitStack
+
+import concourse.mybir as mybir
+
+K, T, D, S, V, N = 1536, 1024, 2, 512, 256, 128
+FLOPS = 2 * K * D * V * N
+
+F32 = mybir.dt.float32
+BF16 = mybir.dt.bfloat16
+U32 = mybir.dt.uint32
+U16 = mybir.dt.uint16
+U8 = mybir.dt.uint8
+FP8X4 = mybir.dt.float8_e4m3fn_x4
+MULT = mybir.AluOpType.mult
+
+P = 128
+PACK = 4
+PASSES = K // (P * PACK)
+HALF = V // 2
+STRETCHES = (
+    ((0, 256, 96), (256, 256, 192), (512, 512, 160)),
+    ((0, 512, 192), (512, 512, 256)),
+    ((0, 512, 288), (512, 256, 192), (768, 256, 160)),
+)
+
+
+def interleave(dst, src):
+    return (
+        dst.rearrange("p (c i) t -> p c t i", i=4),
+        src.rearrange("p t (c i) -> p c t i", i=4),
+    )
+
+
+def tile_picked_tome_lin_none_sub_e_kernel(tc, xT, w, gate, offs, out):
+    nc = tc.nc
+    with ExitStack() as ctx:
+        held = ctx.enter_context(tc.tile_pool(name="held", bufs=1))
+        psum = ctx.enter_context(tc.psum_pool(name="psum", bufs=1))
+
+        offsets = held.tile([P, S // 16], U16, name="offsets")
+        window = held.tile([P, T], F32, name="window", align_bytes=64)
+        gates = held.tile([P, S], F32, name="gates", align_bytes=64)
+
+        scales = held.tile([P, T], U8, name="scales", align_bytes=64)
+        picked_scales = held.tile([P, S], U8, name="picked_scales", align_bytes=64)
+        codes, picked_codes = [], []
+        for a in range(PASSES):
+            codes.append(held.tile([P, T], U32, name=f"codes{a}", align_bytes=64))
+            picked_codes.append(held.tile([P, S], U32, name=f"picked_codes{a}", align_bytes=64))
+        w_grouped = held.tile([P, D * PASSES, N, PACK], BF16, name="w_grouped", align_bytes=64)
+        w_codes = held.tile([P, D * PASSES, N], U32, name="w_codes", align_bytes=64)
+        w_scales = held.tile([P, D * PASSES, N], U8, name="w_scales", align_bytes=64)
+
+        raw = {}
+        for a in range(PASSES):
+            rows = xT[a * P * PACK : (a + 1) * P * PACK, :].rearrange("(p j) t -> p j t", j=PACK)
+            for s, (t0, n, cut) in enumerate(STRETCHES[a]):
+                raw[a, s] = held.tile([P, PACK, n], F32, name=f"raw{a}_{s}", align_bytes=64)
+                nc.sync.dma_start(raw[a, s][:], rows[:, :, t0 : t0 + n])
+                if a == 0 and s == 0:
+                    nc.sync.dma_start(offsets[:], offs)
+        w_rows = w.rearrange("d k m -> (d k) m").rearrange("(u p j) m -> p u j m", p=P, j=PACK)
+        w_raw = {}
+        for u0, u1 in ((0, 2), (2, 4), (4, 5), (5, 6)):
+            tile = held.tile([P, u1 - u0, PACK, N], F32, name=f"w_raw{u0}", align_bytes=64)
+            nc.sync.dma_start(tile[:], w_rows[:, u0:u1, :, :])
+            for u in range(u0, u1):
+                w_raw[u] = tile[:, u - u0, :, :]
+        nc.sync.dma_start(gates[:], gate)
+
+        nc.vector.memset(window[:], 0.0)
+        nc.gpsimd.memset(scales[:], 0)
+
+        grouped = {}
+
+        def cast(a, s):
+            t0, n, cut = STRETCHES[a][s]
+            grouped[a, s] = held.tile([P, n, PACK], BF16, name=f"grouped{a}_{s}", align_bytes=64)
+            nc.scalar.copy(*interleave(grouped[a, s][:, :cut, :], raw[a, s][:, :, :cut]))
+            nc.vector.tensor_copy(*interleave(grouped[a, s][:, cut:, :], raw[a, s][:, :, cut:]))
+
+        def quantise(a, s):
+            t0, n, cut = STRETCHES[a][s]
+            nc.vector.quantize_mx(
+                out=codes[a][:, t0 : t0 + n].bitcast(FP8X4),
+                scales=scales[4 * a :, t0 : t0 + n],
+                in_=grouped[a, s][:].rearrange("p t j -> p (t j)"),
+            )
+
+        def pick_codes(a):
+            nc.vector.tensor_copy(picked_codes[a][:], codes[a][:].indirect(offsets[:]))
+
+        def entries(d, h):
+            return d * V + h * HALF, d * V + (h + 1) * HALF
+
+        def pick_half(picked, table, h):
+            for d in range(D):
+                e0, e1 = entries(d, h)
+                nc.vector.tensor_copy(picked[:, e0:e1], table[:].indirect(offsets[:, e0 // 16 : e1 // 16]))
+
+        def cast_w(u, copy):
+            copy(*interleave(w_grouped[:, u, :, :], w_raw[u]))
+
+        def quantise_w(u0, u1):
+            nc.vector.quantize_mx(
+                out=w_codes[:, u0:u1, :].rearrange("p u m -> p (u m)").bitcast(FP8X4),
+                scales=w_scales[:, u0:u1, :].rearrange("p u m -> p (u m)"),
+                in_=w_grouped[:, u0:u1, :, :].rearrange("p u m j -> p (u m j)"),
+            )
+
+        def multiply(h):
+            acc = psum.tile([P, HALF], F32, name=f"acc{h}")
+            for u in range(D * PASSES):
+                d, a = divmod(u, PASSES)
+                e0, e1 = entries(d, h)
+                nc.tensor.matmul_mx(
+                    out=acc[:],
+                    lhsT=w_codes[:, u, :].bitcast(FP8X4),
+                    lhsT_scale=w_scales[:, u, :],
+                    rhs=picked_codes[a][:, e0:e1].bitcast(FP8X4),
+                    rhs_scale=picked_scales[4 * a :, e0:e1],
+                    start=(u == 0),
+                    stop=(u == D * PASSES - 1),
+                )
+            y = held.tile([P, HALF], F32, name=f"y{h}", align_bytes=64)
+            nc.scalar.copy(y[:], acc[:])
+            return y
+
+        def put_back(y, h):
+            for d in range(D):
+                e0, e1 = entries(d, h)
+                nc.vector.tensor_tensor(
+                    window[:].indirect(offsets[:, e0 // 16 : e1 // 16]), y[:], gates[:, e0:e1], MULT
+                )
+
+        cast(0, 0)
+        cast(0, 1)
+        quantise(0, 0)
+        quantise(0, 1)
+        cast(0, 2)
+        quantise(0, 2)
+        cast(1, 0)
+        pick_codes(0)
+        quantise(1, 0)
+        cast(1, 1)
+        quantise(1, 1)
+        cast(2, 0)
+        pick_codes(1)
+        quantise(2, 0)
+        cast(2, 1)
+        quantise(2, 1)
+        cast(2, 2)
+        quantise(2, 2)
+        for u in range(5):
+            cast_w(u, nc.scalar.copy)
+        pick_half(picked_scales, scales, 0)
+        pick_half(picked_codes[2], codes[2], 0)
+        quantise_w(0, 2)
+        quantise_w(2, 4)
+        cast_w(5, nc.vector.tensor_copy)
+        quantise_w(4, 5)
+        quantise_w(5, 6)
+        y0 = multiply(0)
+        pick_half(picked_scales, scales, 1)
+        pick_half(picked_codes[2], codes[2], 1)
+        y1 = multiply(1)
+        put_back(y0, 0)
+        put_back(y1, 1)
+        nc.sync.dma_start(out, window[:])

@@ -17,10 +17,11 @@ P = 128
 PACK = 4
 PASSES = K // (P * PACK)
 HALF = V // 2
+WHOLE = (True, False, False)
 STRETCHES = (
-    ((0, 256, 96), (256, 256, 192), (512, 512, 160)),
-    ((0, 512, 192), (512, 512, 256)),
-    ((0, 512, 288), (512, 256, 192), (768, 256, 160)),
+    ((0, 512, 224), (512, 512, 224)),
+    ((0, 512, 384), (512, 512, 320)),
+    ((0, 512, 288), (512, 256, 256), (768, 256, 96)),
 )
 
 
@@ -42,23 +43,28 @@ def tile_picked_tome_lin_none_sub_e_kernel(tc, xT, w, gate, offs, out):
         gates = held.tile([P, S], F32, name="gates", align_bytes=64)
 
         scales = held.tile([P, T], U8, name="scales", align_bytes=64)
-        picked_scales = held.tile([P, S], U8, name="picked_scales", align_bytes=64)
-        codes, picked_codes = [], []
-        for a in range(PASSES):
-            codes.append(held.tile([P, T], U32, name=f"codes{a}", align_bytes=64))
-            picked_codes.append(held.tile([P, S], U32, name=f"picked_codes{a}", align_bytes=64))
-        w_grouped = held.tile([P, D * PASSES, N, PACK], BF16, name="w_grouped", align_bytes=64)
+        codes = [held.tile([P, T], U32, name=f"codes{a}", align_bytes=64) for a in range(PASSES)]
+        picked_codes = [held.tile([P, S], U32, name=f"picked_codes{a}", align_bytes=64) for a in range(PASSES - 1)]
+        last_codes, picked_scales = [], []
+        w_grouped = {}
         w_codes = held.tile([P, D * PASSES, N], U32, name="w_codes", align_bytes=64)
         w_scales = held.tile([P, D * PASSES, N], U8, name="w_scales", align_bytes=64)
 
         raw = {}
         for a in range(PASSES):
             rows = xT[a * P * PACK : (a + 1) * P * PACK, :].rearrange("(p j) t -> p j t", j=PACK)
+            if WHOLE[a]:
+                tile = held.tile([P, PACK, T], F32, name=f"raw{a}", align_bytes=64)
+                nc.sync.dma_start(tile[:], rows)
             for s, (t0, n, cut) in enumerate(STRETCHES[a]):
-                raw[a, s] = held.tile([P, PACK, n], F32, name=f"raw{a}_{s}", align_bytes=64)
-                nc.sync.dma_start(raw[a, s][:], rows[:, :, t0 : t0 + n])
-                if a == 0 and s == 0:
-                    nc.sync.dma_start(offsets[:], offs)
+                if WHOLE[a]:
+                    raw[a, s] = tile[:, :, t0 : t0 + n]
+                else:
+                    part = held.tile([P, PACK, n], F32, name=f"raw{a}_{s}", align_bytes=64)
+                    nc.sync.dma_start(part[:], rows[:, :, t0 : t0 + n])
+                    raw[a, s] = part[:]
+            if a == 0:
+                nc.sync.dma_start(offsets[:], offs)
         w_rows = w.rearrange("d k m -> (d k) m").rearrange("(u p j) m -> p u j m", p=P, j=PACK)
         w_raw = {}
         for u0, u1 in ((0, 2), (2, 4), (4, 5), (5, 6)):
@@ -76,8 +82,10 @@ def tile_picked_tome_lin_none_sub_e_kernel(tc, xT, w, gate, offs, out):
         def cast(a, s):
             t0, n, cut = STRETCHES[a][s]
             grouped[a, s] = held.tile([P, n, PACK], BF16, name=f"grouped{a}_{s}", align_bytes=64)
-            nc.scalar.copy(*interleave(grouped[a, s][:, :cut, :], raw[a, s][:, :, :cut]))
-            nc.vector.tensor_copy(*interleave(grouped[a, s][:, cut:, :], raw[a, s][:, :, cut:]))
+            if cut < n:
+                nc.vector.tensor_copy(*interleave(grouped[a, s][:, cut:, :], raw[a, s][:, :, cut:]))
+            if cut > 0:
+                nc.scalar.copy(*interleave(grouped[a, s][:, :cut, :], raw[a, s][:, :, :cut]))
 
         def quantise(a, s):
             t0, n, cut = STRETCHES[a][s]
@@ -96,29 +104,51 @@ def tile_picked_tome_lin_none_sub_e_kernel(tc, xT, w, gate, offs, out):
         def pick_half(picked, table, h):
             for d in range(D):
                 e0, e1 = entries(d, h)
-                nc.vector.tensor_copy(picked[:, e0:e1], table[:].indirect(offsets[:, e0 // 16 : e1 // 16]))
+                nc.vector.tensor_copy(
+                    picked[:, d * HALF : (d + 1) * HALF], table[:].indirect(offsets[:, e0 // 16 : e1 // 16])
+                )
+
+        def pick_last(h):
+            last_codes.append(held.tile([P, V], U32, name=f"last_codes{h}", tag=f"late_codes{h}", align_bytes=64))
+            picked_scales.append(held.tile([P, V], U8, name=f"picked_scales{h}", tag=f"late_scales{h}", align_bytes=64))
+            pick_half(picked_scales[h], scales, h)
+            pick_half(last_codes[h], codes[PASSES - 1], h)
+
+        def group_w(u0, u1, tag):
+            tile = held.tile([P, u1 - u0, N, PACK], BF16, name=f"w_grouped{u0}", tag=tag, align_bytes=64)
+            for u in range(u0, u1):
+                w_grouped[u] = tile[:, u - u0, :, :]
+            w_grouped[u0, u1] = tile[:].rearrange("p u m j -> p (u m j)")
 
         def cast_w(u, copy):
-            copy(*interleave(w_grouped[:, u, :, :], w_raw[u]))
+            copy(*interleave(w_grouped[u], w_raw[u]))
+
+        def cast_w_on_gpsimd(u):
+            nc.gpsimd.tensor_copy(w_grouped[u], w_raw[u].rearrange("p j m -> p m j"))
 
         def quantise_w(u0, u1):
             nc.vector.quantize_mx(
                 out=w_codes[:, u0:u1, :].rearrange("p u m -> p (u m)").bitcast(FP8X4),
                 scales=w_scales[:, u0:u1, :].rearrange("p u m -> p (u m)"),
-                in_=w_grouped[:, u0:u1, :, :].rearrange("p u m j -> p (u m j)"),
+                in_=w_grouped[u0, u1],
             )
+
+        def codes_of(a, d, h):
+            e0, e1 = entries(d, h)
+            if a < PASSES - 1:
+                return picked_codes[a][:, e0:e1]
+            return last_codes[h][:, d * HALF : (d + 1) * HALF]
 
         def multiply(h):
             acc = psum.tile([P, HALF], F32, name=f"acc{h}")
             for u in range(D * PASSES):
                 d, a = divmod(u, PASSES)
-                e0, e1 = entries(d, h)
                 nc.tensor.matmul_mx(
                     out=acc[:],
                     lhsT=w_codes[:, u, :].bitcast(FP8X4),
                     lhsT_scale=w_scales[:, u, :],
-                    rhs=picked_codes[a][:, e0:e1].bitcast(FP8X4),
-                    rhs_scale=picked_scales[4 * a :, e0:e1],
+                    rhs=codes_of(a, d, h).bitcast(FP8X4),
+                    rhs_scale=picked_scales[h][4 * a :, d * HALF : (d + 1) * HALF],
                     start=(u == 0),
                     stop=(u == D * PASSES - 1),
                 )
@@ -137,8 +167,6 @@ def tile_picked_tome_lin_none_sub_e_kernel(tc, xT, w, gate, offs, out):
         cast(0, 1)
         quantise(0, 0)
         quantise(0, 1)
-        cast(0, 2)
-        quantise(0, 2)
         cast(1, 0)
         pick_codes(0)
         quantise(1, 0)
@@ -151,18 +179,23 @@ def tile_picked_tome_lin_none_sub_e_kernel(tc, xT, w, gate, offs, out):
         quantise(2, 1)
         cast(2, 2)
         quantise(2, 2)
-        for u in range(5):
-            cast_w(u, nc.scalar.copy)
-        pick_half(picked_scales, scales, 0)
-        pick_half(picked_codes[2], codes[2], 0)
+        group_w(0, 2, "w_grouped0")
+        group_w(2, 4, "w_grouped2")
+        group_w(4, 5, "late_codes1")
+        group_w(5, 6, "late_scales1")
+        cast_w(0, nc.scalar.copy)
+        cast_w(1, nc.scalar.copy)
+        cast_w(2, nc.scalar.copy)
+        cast_w(3, nc.scalar.copy)
+        cast_w(4, nc.scalar.copy)
+        pick_last(0)
         quantise_w(0, 2)
         quantise_w(2, 4)
         cast_w(5, nc.vector.tensor_copy)
         quantise_w(4, 5)
         quantise_w(5, 6)
         y0 = multiply(0)
-        pick_half(picked_scales, scales, 1)
-        pick_half(picked_codes[2], codes[2], 1)
+        pick_last(1)
         y1 = multiply(1)
         put_back(y0, 0)
         put_back(y1, 1)

from contextlib import ExitStack

import concourse.mybir as mybir

K, T, D, S, V, N = 1536, 1024, 2, 512, 256, 128
FLOPS = 2 * K * D * V * N

F32 = mybir.dt.float32
BF16 = mybir.dt.bfloat16
U32 = mybir.dt.uint32
U16 = mybir.dt.uint16
U8 = mybir.dt.uint8
FP8X4 = mybir.dt.float8_e4m3fn_x4
MULT = mybir.AluOpType.mult

P = 128
PACK = 4
PASSES = K // (P * PACK)
HALF = V // 2
WHOLE = (True, False, False)
STRETCHES = (
    ((0, 512, 224), (512, 512, 224)),
    ((0, 512, 384), (512, 512, 320)),
    ((0, 512, 288), (512, 256, 256), (768, 256, 96)),
)


def interleave(dst, src):
    return (
        dst.rearrange("p (c i) t -> p c t i", i=4),
        src.rearrange("p t (c i) -> p c t i", i=4),
    )


def tile_picked_tome_lin_none_sub_e_kernel(tc, xT, w, gate, offs, out):
    nc = tc.nc
    with ExitStack() as ctx:
        held = ctx.enter_context(tc.tile_pool(name="held", bufs=1))
        psum = ctx.enter_context(tc.psum_pool(name="psum", bufs=1))

        offsets = held.tile([P, S // 16], U16, name="offsets")
        window = held.tile([P, T], F32, name="window", align_bytes=64)
        gates = held.tile([P, S], F32, name="gates", align_bytes=64)

        scales = held.tile([P, T], U8, name="scales", align_bytes=64)
        codes = [held.tile([P, T], U32, name=f"codes{a}", align_bytes=64) for a in range(PASSES)]
        picked_codes = [held.tile([P, S], U32, name=f"picked_codes{a}", align_bytes=64) for a in range(PASSES - 1)]
        last_codes, picked_scales = [], []
        w_grouped = {}
        w_codes = held.tile([P, D * PASSES, N], U32, name="w_codes", align_bytes=64)
        w_scales = held.tile([P, D * PASSES, N], U8, name="w_scales", align_bytes=64)

        raw = {}
        for a in range(PASSES):
            rows = xT[a * P * PACK : (a + 1) * P * PACK, :].rearrange("(p j) t -> p j t", j=PACK)
            if WHOLE[a]:
                tile = held.tile([P, PACK, T], F32, name=f"raw{a}", align_bytes=64)
                nc.sync.dma_start(tile[:], rows)
            for s, (t0, n, cut) in enumerate(STRETCHES[a]):
                if WHOLE[a]:
                    raw[a, s] = tile[:, :, t0 : t0 + n]
                else:
                    part = held.tile([P, PACK, n], F32, name=f"raw{a}_{s}", align_bytes=64)
                    nc.sync.dma_start(part[:], rows[:, :, t0 : t0 + n])
                    raw[a, s] = part[:]
            if a == 0:
                nc.sync.dma_start(offsets[:], offs)
        w_rows = w.rearrange("d k m -> (d k) m").rearrange("(u p j) m -> p u j m", p=P, j=PACK)
        w_raw = {}
        for u0, u1 in ((0, 2), (2, 4), (4, 5), (5, 6)):
            tile = held.tile([P, u1 - u0, PACK, N], F32, name=f"w_raw{u0}", align_bytes=64)
            nc.sync.dma_start(tile[:], w_rows[:, u0:u1, :, :])
            for u in range(u0, u1):
                w_raw[u] = tile[:, u - u0, :, :]
        nc.sync.dma_start(gates[:], gate)

        nc.vector.memset(window[:], 0.0)
        nc.gpsimd.memset(scales[:], 0)

        grouped = {}

        def cast(a, s):
            t0, n, cut = STRETCHES[a][s]
            grouped[a, s] = held.tile([P, n, PACK], BF16, name=f"grouped{a}_{s}", align_bytes=64)
            if cut < n:
                nc.vector.tensor_copy(*interleave(grouped[a, s][:, cut:, :], raw[a, s][:, :, cut:]))
            if cut > 0:
                nc.scalar.copy(*interleave(grouped[a, s][:, :cut, :], raw[a, s][:, :, :cut]))

        def quantise(a, s):
            t0, n, cut = STRETCHES[a][s]
            nc.vector.quantize_mx(
                out=codes[a][:, t0 : t0 + n].bitcast(FP8X4),
                scales=scales[4 * a :, t0 : t0 + n],
                in_=grouped[a, s][:].rearrange("p t j -> p (t j)"),
            )

        def pick_codes(a):
            nc.vector.tensor_copy(picked_codes[a][:], codes[a][:].indirect(offsets[:]))

        def entries(d, h):
            return d * V + h * HALF, d * V + (h + 1) * HALF

        def pick_half(picked, table, h):
            for d in range(D):
                e0, e1 = entries(d, h)
                nc.vector.tensor_copy(
                    picked[:, d * HALF : (d + 1) * HALF], table[:].indirect(offsets[:, e0 // 16 : e1 // 16])
                )

        def pick_last(h):
            last_codes.append(held.tile([P, V], U32, name=f"last_codes{h}", tag=f"late_codes{h}", align_bytes=64))
            picked_scales.append(held.tile([P, V], U8, name=f"picked_scales{h}", tag=f"late_scales{h}", align_bytes=64))
            pick_half(picked_scales[h], scales, h)
            pick_half(last_codes[h], codes[PASSES - 1], h)

        def group_w(u0, u1, tag):
            tile = held.tile([P, u1 - u0, N, PACK], BF16, name=f"w_grouped{u0}", tag=tag, align_bytes=64)
            for u in range(u0, u1):
                w_grouped[u] = tile[:, u - u0, :, :]
            w_grouped[u0, u1] = tile[:].rearrange("p u m j -> p (u m j)")

        def cast_w(u, copy):
            copy(*interleave(w_grouped[u], w_raw[u]))

        def cast_w_on_gpsimd(u):
            nc.gpsimd.tensor_copy(w_grouped[u], w_raw[u].rearrange("p j m -> p m j"))

        def quantise_w(u0, u1):
            nc.vector.quantize_mx(
                out=w_codes[:, u0:u1, :].rearrange("p u m -> p (u m)").bitcast(FP8X4),
                scales=w_scales[:, u0:u1, :].rearrange("p u m -> p (u m)"),
                in_=w_grouped[u0, u1],
            )

        def codes_of(a, d, h):
            e0, e1 = entries(d, h)
            if a < PASSES - 1:
                return picked_codes[a][:, e0:e1]
            return last_codes[h][:, d * HALF : (d + 1) * HALF]

        def multiply(h):
            acc = psum.tile([P, HALF], F32, name=f"acc{h}")
            for u in range(D * PASSES):
                d, a = divmod(u, PASSES)
                nc.tensor.matmul_mx(
                    out=acc[:],
                    lhsT=w_codes[:, u, :].bitcast(FP8X4),
                    lhsT_scale=w_scales[:, u, :],
                    rhs=codes_of(a, d, h).bitcast(FP8X4),
                    rhs_scale=picked_scales[h][4 * a :, d * HALF : (d + 1) * HALF],
                    start=(u == 0),
                    stop=(u == D * PASSES - 1),
                )
            y = held.tile([P, HALF], F32, name=f"y{h}", align_bytes=64)
            nc.scalar.copy(y[:], acc[:])
            return y

        def put_back(y, h):
            for d in range(D):
                e0, e1 = entries(d, h)
                nc.vector.tensor_tensor(
                    window[:].indirect(offsets[:, e0 // 16 : e1 // 16]), y[:], gates[:, e0:e1], MULT
                )

        cast(0, 0)
        cast(0, 1)
        quantise(0, 0)
        quantise(0, 1)
        cast(1, 0)
        pick_codes(0)
        quantise(1, 0)
        cast(1, 1)
        quantise(1, 1)
        cast(2, 0)
        pick_codes(1)
        quantise(2, 0)
        cast(2, 1)
        quantise(2, 1)
        cast(2, 2)
        quantise(2, 2)
        group_w(0, 2, "w_grouped0")
        group_w(2, 4, "w_grouped2")
        group_w(4, 5, "late_codes1")
        group_w(5, 6, "late_scales1")
        cast_w(0, nc.scalar.copy)
        cast_w(1, nc.scalar.copy)
        cast_w(2, nc.scalar.copy)
        cast_w(3, nc.scalar.copy)
        cast_w(4, nc.scalar.copy)
        pick_last(0)
        quantise_w(0, 2)
        quantise_w(2, 4)
        cast_w(5, nc.vector.tensor_copy)
        quantise_w(4, 5)
        quantise_w(5, 6)
        y0 = multiply(0)
        pick_last(1)
        y1 = multiply(1)
        put_back(y0, 0)
        put_back(y1, 1)
        nc.sync.dma_start(out, window[:])
